import numpy as np
import ml_dtypes


def mxq(x, axis, fmt="e4m3"):
    dtype, down = {"e4m3": (ml_dtypes.float8_e4m3fn, 7), "e5m2": (ml_dtypes.float8_e5m2, 14)}[fmt]
    v = np.moveaxis(np.asarray(x, np.float32).astype(ml_dtypes.bfloat16).astype(np.float64), axis, -1)
    blocks = v.reshape(v.shape[:-1] + (-1, 32))
    amax = np.abs(blocks).max(-1, keepdims=True)
    byte = np.maximum(np.where(amax > 0, np.frexp(amax)[1] - 1 + 127, 0) - down, 1)
    scale = np.exp2(byte - 127.0)
    codes = (blocks / scale).astype(np.float32).astype(dtype).astype(np.float64)
    return np.moveaxis((codes * scale).reshape(v.shape), -1, axis)


WIDE = False


def mx_kscale(k):
    if not WIDE:
        return np.ones(k)
    levels = np.array([10, -10, 5, -5, 0])
    if k % 512:
        return np.exp2(np.random.permutation(np.resize(levels, k // 32))).repeat(32)
    a = np.empty((k // 512, 16))
    for p in range(k // 512):
        a[p, :8] = np.random.permutation(np.resize(levels, 8))
        for g in range(8):
            far = levels[np.abs(levels - a[p, g]) >= 10]
            a[p, g + 8] = far[np.random.randint(len(far))]
    return np.exp2(a.ravel()).repeat(32)


def f64(x):
    return np.asarray(x).astype(np.float64)


def striped(idx):
    return np.tile(idx.reshape(-1, 16).T, (8, 1)).astype(np.uint16)


def unstriped(offs):
    return offs[:16].T.reshape(-1).astype(np.int64)


E2M1 = np.array([0.0, 0.5, 1.0, 1.5, 2.0, 3.0, 4.0, 6.0, -0.0, -0.5, -1.0, -1.5, -2.0, -3.0, -4.0, -6.0])


def pack_weight(w, fmt):
    k, n = w.shape
    w = f64(np.asarray(w, np.float32).astype(ml_dtypes.bfloat16)).reshape(k // 32, 32, n)
    amax = np.abs(w).max(1)
    if fmt == "e4m3":
        byte = np.frexp(amax)[1] - 1 + 127 - 7
    else:
        mant, ex = np.frexp(amax / 6.0)
        byte = np.where(mant > 0.5, ex, ex - 1) + 127
    byte = np.clip(np.where(amax > 0, byte, 1), 1, 254)
    scaled = (w * np.exp2(127.0 - byte)[:, None, :]).reshape(k, n).astype(np.float32)
    by_word = np.ascontiguousarray(scaled.reshape(k // 512, 128, 4, n).transpose(0, 1, 3, 2))
    if fmt == "e4m3":
        words = by_word.astype(ml_dtypes.float8_e4m3fn).view(np.uint8)
    else:
        c = by_word.astype(ml_dtypes.float4_e2m1fn).view(np.uint8) & 0xF
        words = (c[..., 0::2] | (c[..., 1::2] << 4)).reshape(k // 512, 128, 2 * n)
    return np.ascontiguousarray(words), np.ascontiguousarray(byte.astype(np.uint8).reshape(k // 512, 16, n))


def unpack_weight(words, scales, fmt):
    g, _, n = scales.shape
    words = np.ascontiguousarray(words).reshape(g, 128, n, -1)
    if fmt == "e4m3":
        vals = words.view(ml_dtypes.float8_e4m3fn).astype(np.float64)
    else:
        nib = np.empty((g, 128, n, 4), np.uint8)
        nib[..., 0::2] = words & 0xF
        nib[..., 1::2] = words >> 4
        vals = E2M1[nib]
    vals = vals * np.repeat(np.exp2(scales.astype(np.float64) - 127.0), 8, axis=1)[..., None]
    return vals.transpose(0, 1, 3, 2).reshape(g * 512, n)


def gelu(v):
    return 0.5 * v * (1.0 + np.tanh(np.sqrt(2.0 / np.pi) * (v + 0.044715 * v**3)))


K, K2, H, N, T, T3, S, T2 = 1024, 512, 1024, 512, 2048, 1024, 512, 1024

def setup_inputs():
    n = np.random.standard_normal
    s = mx_kscale(K)[:, None]
    s2 = mx_kscale(K2)[:, None]
    u = mx_kscale(H)[:, None]
    tab_words, tab_scales = pack_weight(n((K, T)) * s, "e4m3")
    tab2_words, tab2_scales = pack_weight(n((K2, T3)) * s2, "e4m3")
    w1_words, w1_scales = pack_weight(1.2 * n((K, H)) / np.sqrt(K) / s, "e2m1")
    w3_words, w3_scales = pack_weight(n((H, N)) / np.sqrt(H) / u, "e4m3")
    return {
        "tab_words": tab_words, "tab_scales": tab_scales,
        "tab2_words": tab2_words, "tab2_scales": tab2_scales,
        "offs": striped(np.random.permutation(T)[:S]),
        "offs2": striped(np.random.permutation(T3)[:S]),
        "offs3": striped(np.random.permutation(T2)[:S]),
        "offs4": striped(np.random.permutation(T2)[:S]),
        "w1_words": w1_words, "w1_scales": w1_scales,
        "w2": (n((K2, H)) / np.sqrt(K2) / s2 / u.T).astype(np.float32),
        "b2": (0.7 * n(H) / u[:, 0]).astype(np.float32),
        "wg1": np.exp(0.3 * n((128, S))).astype(np.float32),
        "wg2": np.exp(0.3 * n((128, S))).astype(np.float32),
        "quiet": n((H, T2)).astype(np.float32),
        "level": (np.exp(0.3 * n(H)) / u[:, 0]).astype(np.float32),
        "w3_words": w3_words, "w3_scales": w3_scales,
    }

def reference(tab_words, tab_scales, tab2_words, tab2_scales, offs, offs2, offs3, offs4,
              w1_words, w1_scales, w2, b2, wg1, wg2, quiet, level, w3_words, w3_scales):
    v = unpack_weight(tab_words, tab_scales, "e4m3")[:, unstriped(offs)]
    v2 = unpack_weight(tab2_words, tab2_scales, "e4m3")[:, unstriped(offs2)]
    a = unpack_weight(w1_words, w1_scales, "e2m1").T @ v
    h1 = a * np.tanh(a)
    h2 = (mxq(f64(w2), 0, "e4m3").T @ v2) + f64(b2)[:, None]
    pa = np.zeros((H, T2))
    pa[:, unstriped(offs3)] = np.tile(f64(wg1), (H // 128, 1)) * h1
    pb = np.zeros((H, T2))
    pb[:, unstriped(offs4)] = np.tile(f64(wg2), (H // 128, 1)) * h2
    z = (pa + f64(quiet)) / (f64(level)[:, None] + np.abs(pb))
    return unpack_weight(w3_words, w3_scales, "e4m3").T @ mxq(z, 0, "e4m3")

@@ -1,0 +1,324 @@
+from contextlib import ExitStack
+
+import concourse.mybir as mybir
+from concourse.masks import make_identity
+
+K, K2, H, N, T, T3, S, T2 = 1024, 512, 1024, 512, 2048, 1024, 512, 1024
+FLOPS = 2 * (K * H * S + K2 * H * S + H * N * T2)
+
+F32 = mybir.dt.float32
+BF16 = mybir.dt.bfloat16
+I32 = mybir.dt.int32
+U32 = mybir.dt.uint32
+U16 = mybir.dt.uint16
+U8 = mybir.dt.uint8
+FP8X4 = mybir.dt.float8_e4m3fn_x4
+FP4X4 = mybir.dt.float4_e2m1fn_x4
+ACT = mybir.ActivationFunctionType
+MULT = mybir.AluOpType.mult
+
+P = 128
+BANK = 512
+SLICES = H // P
+HALVES = T2 // BANK
+BLOCKS = BANK // P
+LOOP_PAGES = 4
+REGION_PAGES = 3
+RING = 4
+W2_CHUNKS = ((0, 128), (128, 512), (512, 1024))
+
+
+def tile_list_flare_sector_score_kernel(
+    tc, tab_words, tab_scales, tab2_words, tab2_scales, offs, offs2, offs3, offs4,
+    w1_words, w1_scales, w2, b2, wg1, wg2, quiet, level, w3_words, w3_scales, out,
+):
+    nc = tc.nc
+    with ExitStack() as ctx:
+        lists = ctx.enter_context(tc.tile_pool(name="lists", bufs=1))
+        sb = ctx.enter_context(tc.tile_pool(name="sb", bufs=1))
+        ps = ctx.enter_context(tc.psum_pool(name="ps", bufs=1))
+
+        def tiles(name, count, shape, dtype):
+            return [sb.tile(shape, dtype, name="%s%d" % (name, i), align_bytes=64) for i in range(count)]
+
+        def tile(name, shape, dtype):
+            return tiles(name, 1, shape, dtype)[0]
+
+        banks = [ps.tile([P, BANK], F32, name="bank%d" % i) for i in range(8)]
+        turn_banks, root_banks, sum_banks = banks[0:2], banks[2:4], banks[4:8]
+
+        idx = lists.tile([P, S // 16], U16, name="idx")
+        idx2 = lists.tile([P, S // 16], U16, name="idx2")
+        idx3 = lists.tile([P, S // 16], U16, name="idx3")
+        idx4 = lists.tile([P, S // 16], U16, name="idx4")
+
+        v2_words = tile("v2_words", [P, T3], U32)
+        v2_scales = tile("v2_scales", [P, T3], U8)
+        v_words = tiles("v_words", 2, [P, T], U32)
+        v_scales = tile("v_scales", [P, T], U8)
+        w1_codes = tile("w1_codes", [P, 2, 2 * H], U8)
+        w1_plane = tile("w1_plane", [P, 2, H], U8)
+        w3_codes = tile("w3_codes", [P, 2, N], U32)
+        w3_plane = tile("w3_plane", [P, 2, N], U8)
+        g2_words = tile("g2_words", [P, S], U32)
+        g2_scales = tile("g2_scales", [P, S], U8)
+        g_words = tiles("g_words", 2, [P, S], U32)
+        g_scales = tile("g_scales", [P, S], U8)
+        g_scales_moved = tile("g_scales_moved", [P, S], U8)
+        w2_raw = [tile("w2_raw%d_" % c, [P, 4, hi - lo], F32) for c, (lo, hi) in enumerate(W2_CHUNKS)]
+        w2_bf = [tile("w2_bf%d_" % c, [P, hi - lo, 4], BF16) for c, (lo, hi) in enumerate(W2_CHUNKS)]
+        w2_codes = [tile("w2_codes%d_" % c, [P, hi - lo], U32) for c, (lo, hi) in enumerate(W2_CHUNKS)]
+        w2_plane = [tile("w2_plane%d_" % c, [P, hi - lo], U8) for c, (lo, hi) in enumerate(W2_CHUNKS)]
+        wg1_sb = tile("wg1_sb", [P, S], F32)
+        wg2_sb = tile("wg2_sb", [P, S], F32)
+        ident = tile("ident", [P, P], F32)
+        b2_rows = tile("b2_rows", [P, P], F32)
+        level_rows = tile("level_rows", [P, P], F32)
+        b2_cols = tile("b2_cols", [P, SLICES], F32)
+        level_cols = tile("level_cols", [P, SLICES], F32)
+        quiet_sb = tiles("quiet_sb", RING, [P, T2], F32)
+        h2_abs = tiles("h2_abs", LOOP_PAGES, [P, S], F32)
+        h1 = tiles("h1_", SLICES, [P, S], F32)
+        tanh_y = tiles("tanh_y", SLICES, [P, S], F32)
+        loop_pages = tiles("loop_page", LOOP_PAGES, [P, T2], F32)
+        region_pages = tiles("region_page", REGION_PAGES, [P, T2], F32)
+        roots = tiles("root", 2, [P, T2], F32)
+        recips = tiles("recip", RING * HALVES, [P, 2, BLOCKS, 32, 2], F32)
+        z_turned = tiles("z_turned", 2 * HALVES, [P, 2, BLOCKS, 256], BF16)
+        z_pairs = tiles("z_pairs", HALVES, [P, 2 * BANK], F32)
+        z_codes = tiles("z_codes", 2 * HALVES, [P, BANK], U32)
+        z_plane = tiles("z_plane", 2 * HALVES, [P, BANK], U8)
+        staged = tiles("staged", 4 * HALVES, [P, BANK], F32)
+
+        def zero_plane(t):
+            nc.vector.memset(t.bitcast(I32), 0)
+
+        def load_scale_rows(dst_of_quadrant, src_of_quadrant):
+            for q in range(4):
+                nc.sync.dma_start(out=dst_of_quadrant(q).bitcast(I32), in_=src_of_quadrant(q).bitcast(I32))
+
+        def load_words(dst, src):
+            nc.sync.dma_start(out=dst.bitcast(I32), in_=src.bitcast(I32))
+
+        def load_w2(c):
+            lo, hi = W2_CHUNKS[c]
+            nc.sync.dma_start(out=w2_raw[c][:], in_=w2[:, lo:hi].rearrange("(p j) c -> p j c", j=4))
+
+        def load_quiet(s):
+            nc.sync.dma_start(out=quiet_sb[s % RING][:], in_=quiet[s * P : (s + 1) * P, :])
+
+        zero_plane(v2_scales[:])
+        nc.vector.memset(b2_rows[:], 0.0)
+        zero_plane(v_scales[:])
+        zero_plane(w1_plane[:].rearrange("p a c -> p (a c)"))
+        nc.vector.memset(level_rows[:], 0.0)
+        zero_plane(w3_plane[:].rearrange("p a c -> p (a c)"))
+        zero_plane(g_scales_moved[:])
+        make_identity(nc, ident[:])
+        nc.vector.memset(loop_pages[0][:], 0.0)
+        nc.vector.memset(loop_pages[1][:], 0.0)
+        for page in loop_pages[2:] + region_pages:
+            nc.gpsimd.memset(page[:], 0.0)
+
+        nc.sync.dma_start(idx2[:], offs2)
+        load_words(v2_words[:], tab2_words[0].rearrange("p t i -> p (t i)"))
+        load_scale_rows(lambda q: v2_scales[32 * q : 32 * q + 4, :], lambda q: tab2_scales[0, 4 * q : 4 * q + 4, :])
+        load_w2(0)
+        nc.sync.dma_start(out=b2_rows[0:SLICES, :], in_=b2.rearrange("(s p) -> s p", p=P))
+        nc.sync.dma_start(out=wg2_sb[:], in_=wg2)
+        nc.sync.dma_start(idx4[:], offs4)
+        nc.sync.dma_start(idx[:], offs)
+        load_scale_rows(lambda q: v_scales[32 * q : 32 * q + 8, :], lambda q: tab_scales[:, 4 * q : 4 * q + 4, :])
+        load_words(v_words[0][:], tab_words[0].rearrange("p t i -> p (t i)"))
+        load_w2(1)
+        load_words(v_words[1][:], tab_words[1].rearrange("p t i -> p (t i)"))
+        load_words(w1_codes[:], w1_words.rearrange("a p c -> p a c"))
+        load_scale_rows(
+            lambda q: w1_plane[32 * q : 32 * q + 4, :, :],
+            lambda q: w1_scales[:, 4 * q : 4 * q + 4, :].rearrange("a r c -> r a c"),
+        )
+        load_w2(2)
+        nc.sync.dma_start(out=level_rows[0:SLICES, :], in_=level.rearrange("(s p) -> s p", p=P))
+        nc.sync.dma_start(idx3[:], offs3)
+        nc.sync.dma_start(out=wg1_sb[:], in_=wg1)
+        for s in range(RING):
+            load_quiet(s)
+        load_words(w3_codes[:], w3_words.rearrange("a p c i -> p a (c i)"))
+        load_scale_rows(
+            lambda q: w3_plane[32 * q : 32 * q + 4, :, :],
+            lambda q: w3_scales[:, 4 * q : 4 * q + 4, :].rearrange("a r c -> r a c"),
+        )
+
+        def quantize_w2(c):
+            nc.scalar.copy(
+                out=w2_bf[c][:].rearrange("p (c i) j -> p c j i", i=4),
+                in_=w2_raw[c][:].rearrange("p j (c i) -> p c j i", i=4),
+            )
+            nc.vector.quantize_mx(
+                out=w2_codes[c][:].bitcast(FP8X4), scales=w2_plane[c][:], in_=w2_bf[c][:].rearrange("p c j -> p (c j)")
+            )
+
+        def columns_from_rows(cols, rows, bank):
+            nc.tensor.transpose(bank[:, 0:P], rows[:], ident[:])
+            nc.scalar.copy(out=cols[:], in_=bank[:, 0:SLICES])
+
+        def loop_product(s):
+            c = [i for i, (lo, hi) in enumerate(W2_CHUNKS) if lo <= s * P < hi][0]
+            first = s * P - W2_CHUNKS[c][0]
+            bank = turn_banks[s % 2]
+            nc.tensor.matmul_mx(
+                out=bank[:],
+                lhsT=w2_codes[c][:, first : first + P].bitcast(FP8X4),
+                lhsT_scale=w2_plane[c][:, first : first + P],
+                rhs=g2_words[:].bitcast(FP8X4),
+                rhs_scale=g2_scales[:],
+                start=True,
+                stop=True,
+            )
+            nc.scalar.activation(h2_abs[s % LOOP_PAGES][:], bank[:], ACT.Abs, bias=b2_cols[:, s : s + 1])
+
+        def loop_scatter(s):
+            nc.vector.tensor_tensor(
+                loop_pages[s % LOOP_PAGES][:].indirect(idx4[:]), h2_abs[s % LOOP_PAGES][:], wg2_sb[:], MULT
+            )
+
+        def region_product(s):
+            bank = banks[s % 4]
+            for a, plane in enumerate((g_scales, g_scales_moved)):
+                nc.tensor.matmul_mx(
+                    out=bank[:],
+                    lhsT=w1_codes[:, a, 2 * s * P : 2 * (s + 1) * P].bitcast(FP4X4),
+                    lhsT_scale=w1_plane[:, a, s * P : (s + 1) * P],
+                    rhs=g_words[a][:].bitcast(FP8X4),
+                    rhs_scale=plane[:],
+                    start=(a == 0),
+                    stop=(a == 1),
+                )
+            nc.scalar.activation(tanh_y[s][:], bank[:], ACT.Tanh)
+            nc.scalar.copy(out=h1[s][:], in_=bank[:])
+
+        def pair_order(bank):
+            return bank[:].rearrange("p (m q u e) -> p u m q e", m=BLOCKS, u=2, e=2)
+
+        def reciprocal_of_denominator(s):
+            root = roots[s % 2]
+            nc.scalar.activation(
+                root[:], loop_pages[s % LOOP_PAGES][:], ACT.Abs_reciprocal_sqrt, bias=level_cols[:, s : s + 1]
+            )
+            for h in range(HALVES):
+                for m in range(BLOCKS):
+                    first = h * BANK + m * P
+                    nc.tensor.transpose(root_banks[h][:, m * P : (m + 1) * P], root[:, first : first + P], ident[:])
+                nc.scalar.activation(recips[(s % RING) * HALVES + h][:], pair_order(root_banks[h]), ACT.Square)
+
+        def region_scatter(s):
+            nc.vector.tensor_tensor(region_pages[s % REGION_PAGES][:].indirect(idx3[:]), h1[s][:], wg1_sb[:], MULT)
+
+        def quotient(s):
+            terms = (quiet_sb[s % RING], region_pages[s % REGION_PAGES])
+            for h in range(HALVES):
+                bank = sum_banks[(s % 2) * HALVES + h]
+                for term in range(2):
+                    for m in range(BLOCKS):
+                        first = h * BANK + m * P
+                        nc.tensor.matmul(
+                            bank[:, m * P : (m + 1) * P],
+                            lhsT=terms[term][:, first : first + P],
+                            rhs=ident[:],
+                            is_transpose=True,
+                            start=(term == 0 and m == 0),
+                            stop=(term == 1 and m == BLOCKS - 1),
+                        )
+                quarter = s % 4
+                nc.vector.tensor_tensor(
+                    z_turned[(s // 4) * HALVES + h][:, :, :, 64 * quarter : 64 * (quarter + 1)].rearrange(
+                        "p u m (q e) -> p u m q e", e=2
+                    ),
+                    pair_order(bank),
+                    recips[(s % RING) * HALVES + h][:],
+                    MULT,
+                )
+
+        def quantize_z(b, h, two_banks):
+            words = z_turned[b * HALVES + h][:].bitcast(F32)
+            for j, bank in enumerate(two_banks):
+                for k in range(2):
+                    for u in range(2):
+                        first = (2 * k + u) * P
+                        nc.tensor.transpose(bank[:, first : first + P], words[:, u, 2 * j + k, :], ident[:])
+                nc.scalar.copy(
+                    out=z_pairs[h][:, j * BANK : (j + 1) * BANK].rearrange("p (k m u) -> p k m u", k=2, u=2),
+                    in_=bank[:].rearrange("p (k u m) -> p k m u", k=2, u=2),
+                )
+            nc.vector.quantize_mx(
+                out=z_codes[b * HALVES + h][:].bitcast(FP8X4),
+                scales=z_plane[b * HALVES + h][:],
+                in_=z_pairs[h][:].bitcast(BF16),
+            )
+
+        def score_pass(b, h, i, bank):
+            nc.tensor.matmul_mx(
+                out=bank[:],
+                lhsT=w3_codes[:, b, i * P : (i + 1) * P].bitcast(FP8X4),
+                lhsT_scale=w3_plane[:, b, i * P : (i + 1) * P],
+                rhs=z_codes[b * HALVES + h][:].bitcast(FP8X4),
+                rhs_scale=z_plane[b * HALVES + h][:],
+                start=(b == 0),
+                stop=(b == 1),
+            )
+
+        def store_scores(h, i, bank):
+            stage = staged[4 * h + i]
+            if i % 2 == 0:
+                nc.scalar.copy(out=stage[:], in_=bank[:])
+            else:
+                nc.vector.tensor_copy(out=stage[:], in_=bank[:])
+            nc.sync.dma_start(out=out[i * P : (i + 1) * P, h * BANK : (h + 1) * BANK], in_=stage[:])
+
+        nc.vector.tensor_copy(g2_words[:], v2_words[:].indirect(idx2[:]))
+        nc.vector.tensor_copy(g2_scales[:], v2_scales[:].indirect(idx2[:]))
+        quantize_w2(0)
+        columns_from_rows(b2_cols, b2_rows, turn_banks[1])
+        loop_product(0)
+        nc.vector.tensor_copy(g_scales[:], v_scales[:].indirect(idx[:]))
+        nc.gpsimd.dma_start(out=g_scales_moved[0:100, :].bitcast(I32), in_=g_scales[4:104, :].bitcast(I32))
+        loop_scatter(0)
+        for a in range(2):
+            nc.vector.tensor_copy(g_words[a][:], v_words[a][:].indirect(idx[:]))
+        quantize_w2(1)
+        for s in range(1, LOOP_PAGES):
+            loop_product(s)
+            loop_scatter(s)
+        quantize_w2(2)
+        for s in range(SLICES):
+            region_product(s)
+        columns_from_rows(level_cols, level_rows, banks[(SLICES - 1) % 4])
+
+        for s in range(SLICES):
+            nc.vector.tensor_tensor(h1[s][:], h1[s][:], tanh_y[s][:], MULT)
+            region_scatter(s)
+            reciprocal_of_denominator(s)
+            if s + LOOP_PAGES < SLICES:
+                loop_product(s + LOOP_PAGES)
+                loop_scatter(s + LOOP_PAGES)
+            quotient(s)
+            if s + RING < SLICES:
+                load_quiet(s + RING)
+            if s == 3:
+                for h in range(HALVES):
+                    quantize_z(0, h, turn_banks)
+
+        early_banks = root_banks + sum_banks[0:2]
+        late_banks = turn_banks + sum_banks[2:4]
+        for i in range(4):
+            score_pass(0, 0, i, early_banks[i])
+        quantize_z(1, 0, turn_banks)
+        quantize_z(1, 1, sum_banks[2:4])
+        for i in range(4):
+            score_pass(1, 0, i, early_banks[i])
+            store_scores(0, i, early_banks[i])
+        for i in range(4):
+            score_pass(0, 1, i, late_banks[i])
+        for i in range(4):
+            score_pass(1, 1, i, late_banks[i])
+            store_scores(1, i, late_banks[i])

@@ -16,16 +16,19 @@ FP8X4 = mybir.dt.float8_e4m3fn_x4
 FP4X4 = mybir.dt.float4_e2m1fn_x4
 ACT = mybir.ActivationFunctionType
 MULT = mybir.AluOpType.mult
+ADD = mybir.AluOpType.add
 
 P = 128
 BANK = 512
 SLICES = H // P
 HALVES = T2 // BANK
 BLOCKS = BANK // P
-LOOP_PAGES = 4
-REGION_PAGES = 3
+REGION_PAGES = 2
 RING = 4
-W2_CHUNKS = ((0, 128), (128, 512), (512, 1024))
+W2_CHUNKS = ((0, 128), (128, 256), (256, 512), (512, 1024))
+KIB = 1024
+LEAD = 3
+REGION_BANKS = (4, 5, 6, 7)
 
 
 def tile_list_flare_sector_score_kernel(
@@ -36,6 +39,7 @@ def tile_list_flare_sector_score_kernel(
     with ExitStack() as ctx:
         lists = ctx.enter_context(tc.tile_pool(name="lists", bufs=1))
         sb = ctx.enter_context(tc.tile_pool(name="sb", bufs=1))
+        reused = ctx.enter_context(tc.tile_pool(name="reused", bufs=1))
         ps = ctx.enter_context(tc.psum_pool(name="ps", bufs=1))
 
         def tiles(name, count, shape, dtype):
@@ -52,23 +56,39 @@ def tile_list_flare_sector_score_kernel(
         idx3 = lists.tile([P, S // 16], U16, name="idx3")
         idx4 = lists.tile([P, S // 16], U16, name="idx4")
 
+        def placed(name, shape, dtype, kib):
+            return reused.tile(shape, dtype, name=name, align_bytes=64, offset=kib * KIB)
+
+        widths = [hi - lo for lo, hi in W2_CHUNKS]
+        loop_pages = [placed("loop_page%d" % s, [P, T2], F32, 4 * s) for s in range(SLICES)]
+        region_pages = [placed("region_page%d" % i, [P, T2], F32, (128, 52)[i]) for i in range(REGION_PAGES)]
+        v_scales = placed("v_scales", [P, T], U8, 12)
+        w2_codes = [placed("w2_codes%d" % c, [P, widths[c]], U32, (16, 24, 60, 52)[c]) for c in range(4)]
+        w2_plane = [placed("w2_plane%d" % c, [P, widths[c]], U8, (20, 28, 61, 62)[c]) for c in range(4)]
+        w1_codes = placed("w1_codes", [P, 2, 2 * H], U8, 32)
+        g_words = [placed("g_words%d" % a, [P, S], U32, 36 + 2 * a) for a in range(2)]
+        v_words = [placed("v_words%d" % a, [P, T], U32, 40 + 8 * a) for a in range(2)]
+        h2_abs = [placed("h2_abs%d" % s, [P, S], F32, {2: 48, 3: 50}.get(s, 64 + 2 * s)) for s in range(SLICES)]
+        quiet_sb = [placed("quiet_sb%d" % i, [P, T2], F32, (40, 44, 56, 68)[i]) for i in range(RING)]
+        h1 = placed("h1", [P, S], F32, 64 + 2 * (SLICES - 1))
+        recips = [placed("recip%d" % i, [P, 2, BLOCKS, 32, 2], F32, 80 + 2 * i) for i in range(SLICES * HALVES)]
+        z_turned = [placed("z_turned%d" % i, [P, 2, BLOCKS, 256], BF16, (32, 36, 0, 4)[i]) for i in range(2 * HALVES)]
+        tanh_y = [placed("tanh_y%d" % s, [P, S], F32, 112 + 2 * s) for s in range(SLICES)]
+        staged = [placed("staged%d" % s, [P, BANK], F32, 112 + 2 * s) for s in range(4 * HALVES)]
+
+        w2_raw = [tile("w2_raw%d_" % c, [P, 4, widths[c]], F32) for c in range(4)]
+        w2_bf = [tile("w2_bf%d_" % c, [P, widths[c], 4], BF16) for c in range(3)]
+        w2_bf.append(placed("w2_bf3", [P, widths[3], 4], BF16, 128))
+        first_pass = tiles("first_pass", 4, [P, BANK], F32)
         v2_words = tile("v2_words", [P, T3], U32)
         v2_scales = tile("v2_scales", [P, T3], U8)
-        v_words = tiles("v_words", 2, [P, T], U32)
-        v_scales = tile("v_scales", [P, T], U8)
-        w1_codes = tile("w1_codes", [P, 2, 2 * H], U8)
         w1_plane = tile("w1_plane", [P, 2, H], U8)
         w3_codes = tile("w3_codes", [P, 2, N], U32)
         w3_plane = tile("w3_plane", [P, 2, N], U8)
         g2_words = tile("g2_words", [P, S], U32)
         g2_scales = tile("g2_scales", [P, S], U8)
-        g_words = tiles("g_words", 2, [P, S], U32)
         g_scales = tile("g_scales", [P, S], U8)
         g_scales_moved = tile("g_scales_moved", [P, S], U8)
-        w2_raw = [tile("w2_raw%d_" % c, [P, 4, hi - lo], F32) for c, (lo, hi) in enumerate(W2_CHUNKS)]
-        w2_bf = [tile("w2_bf%d_" % c, [P, hi - lo, 4], BF16) for c, (lo, hi) in enumerate(W2_CHUNKS)]
-        w2_codes = [tile("w2_codes%d_" % c, [P, hi - lo], U32) for c, (lo, hi) in enumerate(W2_CHUNKS)]
-        w2_plane = [tile("w2_plane%d_" % c, [P, hi - lo], U8) for c, (lo, hi) in enumerate(W2_CHUNKS)]
         wg1_sb = tile("wg1_sb", [P, S], F32)
         wg2_sb = tile("wg2_sb", [P, S], F32)
         ident = tile("ident", [P, P], F32)
@@ -76,19 +96,11 @@ def tile_list_flare_sector_score_kernel(
         level_rows = tile("level_rows", [P, P], F32)
         b2_cols = tile("b2_cols", [P, SLICES], F32)
         level_cols = tile("level_cols", [P, SLICES], F32)
-        quiet_sb = tiles("quiet_sb", RING, [P, T2], F32)
-        h2_abs = tiles("h2_abs", LOOP_PAGES, [P, S], F32)
-        h1 = tiles("h1_", SLICES, [P, S], F32)
-        tanh_y = tiles("tanh_y", SLICES, [P, S], F32)
-        loop_pages = tiles("loop_page", LOOP_PAGES, [P, T2], F32)
-        region_pages = tiles("region_page", REGION_PAGES, [P, T2], F32)
+        y = tiles("y", SLICES, [P, S], F32)
         roots = tiles("root", 2, [P, T2], F32)
-        recips = tiles("recip", RING * HALVES, [P, 2, BLOCKS, 32, 2], F32)
-        z_turned = tiles("z_turned", 2 * HALVES, [P, 2, BLOCKS, 256], BF16)
         z_pairs = tiles("z_pairs", HALVES, [P, 2 * BANK], F32)
         z_codes = tiles("z_codes", 2 * HALVES, [P, BANK], U32)
         z_plane = tiles("z_plane", 2 * HALVES, [P, BANK], U8)
-        staged = tiles("staged", 4 * HALVES, [P, BANK], F32)
 
         def zero_plane(t):
             nc.vector.memset(t.bitcast(I32), 0)
@@ -107,42 +119,44 @@ def tile_list_flare_sector_score_kernel(
         def load_quiet(s):
             nc.sync.dma_start(out=quiet_sb[s % RING][:], in_=quiet[s * P : (s + 1) * P, :])
 
-        zero_plane(v2_scales[:])
-        nc.vector.memset(b2_rows[:], 0.0)
-        zero_plane(v_scales[:])
-        zero_plane(w1_plane[:].rearrange("p a c -> p (a c)"))
-        nc.vector.memset(level_rows[:], 0.0)
-        zero_plane(w3_plane[:].rearrange("p a c -> p (a c)"))
-        zero_plane(g_scales_moved[:])
+        nc.gpsimd.memset(v_scales[:].bitcast(I32), 0)
         make_identity(nc, ident[:])
-        nc.vector.memset(loop_pages[0][:], 0.0)
-        nc.vector.memset(loop_pages[1][:], 0.0)
-        for page in loop_pages[2:] + region_pages:
-            nc.gpsimd.memset(page[:], 0.0)
+        zero_plane(w1_plane[:].rearrange("p a c -> p (a c)"))
+        zero_plane(g_scales_moved[:])
+        zero_plane(w3_plane[:].rearrange("p a c -> p (a c)"))
+        for page in loop_pages[0:3]:
+            nc.vector.memset(page[:], 0.0)
+
+        def load_rows_on_all_partitions(rows, vector):
+            nc.sync.dma_start(
+                out=rows[:], in_=vector.rearrange("(s p) -> s p", p=P).unsqueeze(0).to_broadcast([P // SLICES, SLICES, P])
+            )
 
         nc.sync.dma_start(idx2[:], offs2)
+        load_scale_rows(
+            lambda q: v2_scales[32 * q : 32 * (q + 1), :],
+            lambda q: tab2_scales[0, 4 * q : 4 * q + 4, :].unsqueeze(0).to_broadcast([8, 4, T3]),
+        )
         load_words(v2_words[:], tab2_words[0].rearrange("p t i -> p (t i)"))
-        load_scale_rows(lambda q: v2_scales[32 * q : 32 * q + 4, :], lambda q: tab2_scales[0, 4 * q : 4 * q + 4, :])
         load_w2(0)
-        nc.sync.dma_start(out=b2_rows[0:SLICES, :], in_=b2.rearrange("(s p) -> s p", p=P))
-        nc.sync.dma_start(out=wg2_sb[:], in_=wg2)
-        nc.sync.dma_start(idx4[:], offs4)
+        load_rows_on_all_partitions(b2_rows, b2)
+        load_w2(1)
         nc.sync.dma_start(idx[:], offs)
         load_scale_rows(lambda q: v_scales[32 * q : 32 * q + 8, :], lambda q: tab_scales[:, 4 * q : 4 * q + 4, :])
+        nc.sync.dma_start(out=wg2_sb[:], in_=wg2)
+        nc.sync.dma_start(idx4[:], offs4)
+        load_w2(2)
+        load_w2(3)
         load_words(v_words[0][:], tab_words[0].rearrange("p t i -> p (t i)"))
-        load_w2(1)
         load_words(v_words[1][:], tab_words[1].rearrange("p t i -> p (t i)"))
         load_words(w1_codes[:], w1_words.rearrange("a p c -> p a c"))
         load_scale_rows(
             lambda q: w1_plane[32 * q : 32 * q + 4, :, :],
             lambda q: w1_scales[:, 4 * q : 4 * q + 4, :].rearrange("a r c -> r a c"),
         )
-        load_w2(2)
-        nc.sync.dma_start(out=level_rows[0:SLICES, :], in_=level.rearrange("(s p) -> s p", p=P))
+        load_rows_on_all_partitions(level_rows, level)
         nc.sync.dma_start(idx3[:], offs3)
         nc.sync.dma_start(out=wg1_sb[:], in_=wg1)
-        for s in range(RING):
-            load_quiet(s)
         load_words(w3_codes[:], w3_words.rearrange("a p c i -> p a (c i)"))
         load_scale_rows(
             lambda q: w3_plane[32 * q : 32 * q + 4, :, :],
@@ -175,15 +189,15 @@ def tile_list_flare_sector_score_kernel(
                 start=True,
                 stop=True,
             )
-            nc.scalar.activation(h2_abs[s % LOOP_PAGES][:], bank[:], ACT.Abs, bias=b2_cols[:, s : s + 1])
+            nc.scalar.activation(h2_abs[s][:], bank[:], ACT.Abs, bias=b2_cols[:, s : s + 1])
 
         def loop_scatter(s):
             nc.vector.tensor_tensor(
-                loop_pages[s % LOOP_PAGES][:].indirect(idx4[:]), h2_abs[s % LOOP_PAGES][:], wg2_sb[:], MULT
+                loop_pages[s][:].indirect(idx4[:]), h2_abs[s][:], wg2_sb[:], MULT
             )
 
         def region_product(s):
-            bank = banks[s % 4]
+            bank = banks[REGION_BANKS[s % len(REGION_BANKS)]]
             for a, plane in enumerate((g_scales, g_scales_moved)):
                 nc.tensor.matmul_mx(
                     out=bank[:],
@@ -195,29 +209,30 @@ def tile_list_flare_sector_score_kernel(
                     stop=(a == 1),
                 )
             nc.scalar.activation(tanh_y[s][:], bank[:], ACT.Tanh)
-            nc.scalar.copy(out=h1[s][:], in_=bank[:])
+            nc.scalar.copy(out=y[s][:], in_=bank[:])
 
         def pair_order(bank):
             return bank[:].rearrange("p (m q u e) -> p u m q e", m=BLOCKS, u=2, e=2)
 
         def reciprocal_of_denominator(s):
             root = roots[s % 2]
+            pair = sum_banks[0:2] if s == LEAD else root_banks
             nc.scalar.activation(
-                root[:], loop_pages[s % LOOP_PAGES][:], ACT.Abs_reciprocal_sqrt, bias=level_cols[:, s : s + 1]
+                root[:], loop_pages[s][:], ACT.Abs_reciprocal_sqrt, bias=level_cols[:, s : s + 1]
             )
             for h in range(HALVES):
                 for m in range(BLOCKS):
                     first = h * BANK + m * P
-                    nc.tensor.transpose(root_banks[h][:, m * P : (m + 1) * P], root[:, first : first + P], ident[:])
-                nc.scalar.activation(recips[(s % RING) * HALVES + h][:], pair_order(root_banks[h]), ACT.Square)
+                    nc.tensor.transpose(pair[h][:, m * P : (m + 1) * P], root[:, first : first + P], ident[:])
+                nc.scalar.activation(recips[s * HALVES + h][:], pair_order(pair[h]), ACT.Square)
 
         def region_scatter(s):
-            nc.vector.tensor_tensor(region_pages[s % REGION_PAGES][:].indirect(idx3[:]), h1[s][:], wg1_sb[:], MULT)
+            nc.vector.tensor_copy(region_pages[s % REGION_PAGES][:].indirect(idx3[:]), y[s][:])
 
         def quotient(s):
             terms = (quiet_sb[s % RING], region_pages[s % REGION_PAGES])
             for h in range(HALVES):
-                bank = sum_banks[(s % 2) * HALVES + h]
+                bank = sum_banks[(HALVES if s == SLICES - 1 else 0) + h]
                 for term in range(2):
                     for m in range(BLOCKS):
                         first = h * BANK + m * P
@@ -235,18 +250,18 @@ def tile_list_flare_sector_score_kernel(
                         "p u m (q e) -> p u m q e", e=2
                     ),
                     pair_order(bank),
-                    recips[(s % RING) * HALVES + h][:],
+                    recips[s * HALVES + h][:],
                     MULT,
                 )
 
-        def quantize_z(b, h, two_banks):
+        def quantize_z(b, h, two_banks, copies):
             words = z_turned[b * HALVES + h][:].bitcast(F32)
             for j, bank in enumerate(two_banks):
                 for k in range(2):
                     for u in range(2):
                         first = (2 * k + u) * P
                         nc.tensor.transpose(bank[:, first : first + P], words[:, u, 2 * j + k, :], ident[:])
-                nc.scalar.copy(
+                copies[j](
                     out=z_pairs[h][:, j * BANK : (j + 1) * BANK].rearrange("p (k m u) -> p k m u", k=2, u=2),
                     in_=bank[:].rearrange("p (k u m) -> p k m u", k=2, u=2),
                 )
@@ -256,69 +271,83 @@ def tile_list_flare_sector_score_kernel(
                 in_=z_pairs[h][:].bitcast(BF16),
             )
 
-        def score_pass(b, h, i, bank):
+        def score_pass(b, h, i, bank, start, stop):
             nc.tensor.matmul_mx(
                 out=bank[:],
                 lhsT=w3_codes[:, b, i * P : (i + 1) * P].bitcast(FP8X4),
                 lhsT_scale=w3_plane[:, b, i * P : (i + 1) * P],
                 rhs=z_codes[b * HALVES + h][:].bitcast(FP8X4),
                 rhs_scale=z_plane[b * HALVES + h][:],
-                start=(b == 0),
-                stop=(b == 1),
+                start=start,
+                stop=stop,
             )
 
-        def store_scores(h, i, bank):
-            stage = staged[4 * h + i]
-            if i % 2 == 0:
-                nc.scalar.copy(out=stage[:], in_=bank[:])
-            else:
-                nc.vector.tensor_copy(out=stage[:], in_=bank[:])
-            nc.sync.dma_start(out=out[i * P : (i + 1) * P, h * BANK : (h + 1) * BANK], in_=stage[:])
+        def store_scores(h, i):
+            nc.sync.dma_start(out=out[i * P : (i + 1) * P, h * BANK : (h + 1) * BANK], in_=staged[4 * h + i][:])
 
-        nc.vector.tensor_copy(g2_words[:], v2_words[:].indirect(idx2[:]))
         nc.vector.tensor_copy(g2_scales[:], v2_scales[:].indirect(idx2[:]))
+        nc.vector.tensor_copy(g2_words[:], v2_words[:].indirect(idx2[:]))
         quantize_w2(0)
         columns_from_rows(b2_cols, b2_rows, turn_banks[1])
         loop_product(0)
+        quantize_w2(1)
+        loop_product(1)
         nc.vector.tensor_copy(g_scales[:], v_scales[:].indirect(idx[:]))
         nc.gpsimd.dma_start(out=g_scales_moved[0:100, :].bitcast(I32), in_=g_scales[4:104, :].bitcast(I32))
+        for page in loop_pages[3:]:
+            nc.gpsimd.memset(page[:], 0.0)
         loop_scatter(0)
+        loop_scatter(1)
+        quantize_w2(2)
         for a in range(2):
             nc.vector.tensor_copy(g_words[a][:], v_words[a][:].indirect(idx[:]))
-        quantize_w2(1)
-        for s in range(1, LOOP_PAGES):
+        quantize_w2(3)
+        for s in range(2, SLICES):
             loop_product(s)
             loop_scatter(s)
-        quantize_w2(2)
+        for page in region_pages:
+            nc.gpsimd.memset(page[:], 0.0)
         for s in range(SLICES):
             region_product(s)
-        columns_from_rows(level_cols, level_rows, banks[(SLICES - 1) % 4])
-
         for s in range(SLICES):
-            nc.vector.tensor_tensor(h1[s][:], h1[s][:], tanh_y[s][:], MULT)
-            region_scatter(s)
+            engine = nc.vector if s == 0 else nc.gpsimd
+            engine.tensor_tensor(h1[:], y[s][:], tanh_y[s][:], MULT)
+            engine.tensor_tensor(y[s][:], h1[:], wg1_sb[:], MULT)
+        columns_from_rows(level_cols, level_rows, banks[REGION_BANKS[(SLICES - 1) % len(REGION_BANKS)]])
+        for s in range(RING):
+            load_quiet(s)
+        scalar_copies = (nc.scalar.copy, nc.scalar.copy)
+        held_banks = root_banks + turn_banks
+
+        for s in range(LEAD + 1):
             reciprocal_of_denominator(s)
-            if s + LOOP_PAGES < SLICES:
-                loop_product(s + LOOP_PAGES)
-                loop_scatter(s + LOOP_PAGES)
+        region_scatter(0)
+        for s in range(SLICES):
+            if s + 1 < SLICES:
+                region_scatter(s + 1)
+            if s + LEAD + 1 < SLICES:
+                reciprocal_of_denominator(s + LEAD + 1)
             quotient(s)
             if s + RING < SLICES:
                 load_quiet(s + RING)
             if s == 3:
                 for h in range(HALVES):
-                    quantize_z(0, h, turn_banks)
+                    quantize_z(0, h, turn_banks, scalar_copies)
+            if s == 4:
+                for i in range(4):
+                    score_pass(0, 1, i, sum_banks[2 + i % 2], True, True)
+                    nc.scalar.copy(out=first_pass[i][:], in_=sum_banks[2 + i % 2][:])
+            if s == 5:
+                for i in range(4):
+                    score_pass(0, 0, i, held_banks[i], True, False)
 
-        early_banks = root_banks + sum_banks[0:2]
-        late_banks = turn_banks + sum_banks[2:4]
+        quantize_z(1, 0, sum_banks[0:2], (nc.scalar.copy, nc.vector.tensor_copy))
+        quantize_z(1, 1, sum_banks[2:4], scalar_copies)
         for i in range(4):
-            score_pass(0, 0, i, early_banks[i])
-        quantize_z(1, 0, turn_banks)
-        quantize_z(1, 1, sum_banks[2:4])
+            score_pass(1, 0, i, held_banks[i], False, True)
+            nc.scalar.copy(out=staged[i][:], in_=held_banks[i][:])
+            store_scores(0, i)
         for i in range(4):
-            score_pass(1, 0, i, early_banks[i])
-            store_scores(0, i, early_banks[i])
-        for i in range(4):
-            score_pass(0, 1, i, late_banks[i])
-        for i in range(4):
-            score_pass(1, 1, i, late_banks[i])
-            store_scores(1, i, late_banks[i])
+            score_pass(1, 1, i, sum_banks[i], True, True)
+            nc.vector.tensor_tensor(staged[4 + i][:], sum_banks[i][:], first_pass[i][:], ADD)
+            store_scores(1, i)

@@ -27,8 +27,11 @@ REGION_PAGES = 2
 RING = 4
 W2_CHUNKS = ((0, 128), (128, 256), (256, 512), (512, 1024))
 KIB = 1024
+AHEAD = 4
+FUSED = 3
+POOL_SLICES = (0, 1, 2, 3, 4, 5)
 LEAD = 3
-REGION_BANKS = (4, 5, 6, 7)
+REGION_BANKS = (2, 3, 6, 7)
 
 
 def tile_list_flare_sector_score_kernel(
@@ -60,25 +63,29 @@ def tile_list_flare_sector_score_kernel(
             return reused.tile(shape, dtype, name=name, align_bytes=64, offset=kib * KIB)
 
         widths = [hi - lo for lo, hi in W2_CHUNKS]
-        loop_pages = [placed("loop_page%d" % s, [P, T2], F32, 4 * s) for s in range(SLICES)]
-        region_pages = [placed("region_page%d" % i, [P, T2], F32, (128, 52)[i]) for i in range(REGION_PAGES)]
+        loop_pages = [placed("loop_page%d" % s, [P, T2], F32, 4 * s) for s in range(4)]
+        region_pages = [placed("region_page%d" % i, [P, T2], F32, (56, 128)[i]) for i in range(REGION_PAGES)]
         v_scales = placed("v_scales", [P, T], U8, 12)
-        w2_codes = [placed("w2_codes%d" % c, [P, widths[c]], U32, (16, 24, 60, 52)[c]) for c in range(4)]
-        w2_plane = [placed("w2_plane%d" % c, [P, widths[c]], U8, (20, 28, 61, 62)[c]) for c in range(4)]
+        w2_codes = [placed("w2_codes%d" % c, [P, widths[c]], U32, (57, 129, 60, 52)[c]) for c in range(4)]
+        w2_plane = [placed("w2_plane%d" % c, [P, widths[c]], U8, (56, 128, 61, 62)[c]) for c in range(4)]
         w1_codes = placed("w1_codes", [P, 2, 2 * H], U8, 32)
         g_words = [placed("g_words%d" % a, [P, S], U32, 36 + 2 * a) for a in range(2)]
         v_words = [placed("v_words%d" % a, [P, T], U32, 40 + 8 * a) for a in range(2)]
-        h2_abs = [placed("h2_abs%d" % s, [P, S], F32, {2: 48, 3: 50}.get(s, 64 + 2 * s)) for s in range(SLICES)]
-        quiet_sb = [placed("quiet_sb%d" % i, [P, T2], F32, (40, 44, 56, 68)[i]) for i in range(RING)]
-        h1 = placed("h1", [P, S], F32, 64 + 2 * (SLICES - 1))
+        abs_kib = [{2: 48, 3: 50}.get(s, 64 + 2 * s) for s in range(SLICES)]
+        h2_abs = [placed("h2_abs%d" % s, [P, S], F32, abs_kib[s]) for s in range(SLICES)]
+        pb_values = {s: placed("pb_values%d" % s, [P, S], F32, 112 + 2 * 3 if s == FUSED + 1 else abs_kib[s - 1]) for s in range(FUSED, SLICES)}
+        quiet_sb = [placed("quiet_sb%d" % i, [P, T2], F32, (40, 44, 132, 68)[i]) for i in range(RING)]
+        h1_first = placed("h1_first", [P, S], F32, abs_kib[FUSED])
+        h1 = [h1_first] * 5 + [placed("h1_5", [P, S], F32, 112 + 2 * 4)] + [placed("h1_last", [P, S], F32, 16 + 2 * 6)] * 2
+        pa_values = [placed("pa_values%d" % s, [P, S], F32, {6: 16 + 2 * 7}.get(s, 138 + 2 * s)) for s in range(SLICES)]
+        numerators = [placed("numerator%d" % i, [P, 2, BLOCKS, 32, 2], F32, 16 + 2 * i) for i in range(8)]
         recips = [placed("recip%d" % i, [P, 2, BLOCKS, 32, 2], F32, 80 + 2 * i) for i in range(SLICES * HALVES)]
         z_turned = [placed("z_turned%d" % i, [P, 2, BLOCKS, 256], BF16, (32, 36, 0, 4)[i]) for i in range(2 * HALVES)]
         tanh_y = [placed("tanh_y%d" % s, [P, S], F32, 112 + 2 * s) for s in range(SLICES)]
         staged = [placed("staged%d" % s, [P, BANK], F32, 112 + 2 * s) for s in range(4 * HALVES)]
 
         w2_raw = [tile("w2_raw%d_" % c, [P, 4, widths[c]], F32) for c in range(4)]
-        w2_bf = [tile("w2_bf%d_" % c, [P, widths[c], 4], BF16) for c in range(3)]
-        w2_bf.append(placed("w2_bf3", [P, widths[3], 4], BF16, 128))
+        w2_bf = [tile("w2_bf%d_" % c, [P, widths[c], 4], BF16) for c in range(4)]
         first_pass = tiles("first_pass", 4, [P, BANK], F32)
         v2_words = tile("v2_words", [P, T3], U32)
         v2_scales = tile("v2_scales", [P, T3], U8)
@@ -96,10 +103,11 @@ def tile_list_flare_sector_score_kernel(
         level_rows = tile("level_rows", [P, P], F32)
         b2_cols = tile("b2_cols", [P, SLICES], F32)
         level_cols = tile("level_cols", [P, SLICES], F32)
-        y = tiles("y", SLICES, [P, S], F32)
+        y = [placed("y%d" % s, [P, S], F32, 138 + 2 * s) for s in range(SLICES)]
         roots = tiles("root", 2, [P, T2], F32)
         z_pairs = tiles("z_pairs", HALVES, [P, 2 * BANK], F32)
-        z_codes = tiles("z_codes", 2 * HALVES, [P, BANK], U32)
+        z_codes = [placed("z_codes0", [P, BANK], U32, 138 + 2 * 5), placed("z_codes1", [P, BANK], U32, 16 + 2 * 7)]
+        z_codes = z_codes + tiles("z_codes_last", HALVES, [P, BANK], U32)
         z_plane = tiles("z_plane", 2 * HALVES, [P, BANK], U8)
 
         def zero_plane(t):
@@ -191,10 +199,15 @@ def tile_list_flare_sector_score_kernel(
             )
             nc.scalar.activation(h2_abs[s][:], bank[:], ACT.Abs, bias=b2_cols[:, s : s + 1])
 
+        def loop_values(s):
+            engine = nc.vector if s == FUSED else nc.gpsimd
+            engine.tensor_tensor(pb_values[s][:], h2_abs[s][:], wg2_sb[:], MULT)
+
         def loop_scatter(s):
-            nc.vector.tensor_tensor(
-                loop_pages[s][:].indirect(idx4[:]), h2_abs[s][:], wg2_sb[:], MULT
-            )
+            if s < FUSED:
+                nc.vector.tensor_tensor(loop_pages[s % 4][:].indirect(idx4[:]), h2_abs[s][:], wg2_sb[:], MULT)
+            else:
+                nc.vector.tensor_copy(loop_pages[s % 4][:].indirect(idx4[:]), pb_values[s][:])
 
         def region_product(s):
             bank = banks[REGION_BANKS[s % len(REGION_BANKS)]]
@@ -216,9 +229,9 @@ def tile_list_flare_sector_score_kernel(
 
         def reciprocal_of_denominator(s):
             root = roots[s % 2]
-            pair = sum_banks[0:2] if s == LEAD else root_banks
+            pair = sum_banks[0:2] if s % 4 == 3 else root_banks
             nc.scalar.activation(
-                root[:], loop_pages[s][:], ACT.Abs_reciprocal_sqrt, bias=level_cols[:, s : s + 1]
+                root[:], loop_pages[s % 4][:], ACT.Abs_reciprocal_sqrt, bias=level_cols[:, s : s + 1]
             )
             for h in range(HALVES):
                 for m in range(BLOCKS):
@@ -226,10 +239,20 @@ def tile_list_flare_sector_score_kernel(
                     nc.tensor.transpose(pair[h][:, m * P : (m + 1) * P], root[:, first : first + P], ident[:])
                 nc.scalar.activation(recips[s * HALVES + h][:], pair_order(pair[h]), ACT.Square)
 
-        def region_scatter(s):
-            nc.vector.tensor_copy(region_pages[s % REGION_PAGES][:].indirect(idx3[:]), y[s][:])
+        def region_h1(s):
+            nc.gpsimd.tensor_tensor(h1[s][:], y[s][:], tanh_y[s][:], MULT)
 
-        def quotient(s):
+        def region_weighted(s):
+            nc.gpsimd.tensor_tensor(pa_values[s][:], h1[s][:], wg1_sb[:], MULT)
+
+        def region_values(s):
+            region_h1(s)
+            region_weighted(s)
+
+        def region_scatter(s):
+            nc.vector.tensor_copy(region_pages[s % REGION_PAGES][:].indirect(idx3[:]), pa_values[s][:])
+
+        def numerator_sum(s):
             terms = (quiet_sb[s % RING], region_pages[s % REGION_PAGES])
             for h in range(HALVES):
                 bank = sum_banks[(HALVES if s == SLICES - 1 else 0) + h]
@@ -244,15 +267,23 @@ def tile_list_flare_sector_score_kernel(
                             start=(term == 0 and m == 0),
                             stop=(term == 1 and m == BLOCKS - 1),
                         )
+                if s in POOL_SLICES:
+                    nc.scalar.copy(out=numerators[(s * HALVES + h) % 8][:], in_=pair_order(bank))
+            if s + RING < SLICES:
+                load_quiet(s + RING)
+
+        def quotient(s, halves=(0, 1)):
+            for h in halves:
+                bank = sum_banks[(HALVES if s == SLICES - 1 else 0) + h]
                 quarter = s % 4
-                nc.vector.tensor_tensor(
-                    z_turned[(s // 4) * HALVES + h][:, :, :, 64 * quarter : 64 * (quarter + 1)].rearrange(
-                        "p u m (q e) -> p u m q e", e=2
-                    ),
-                    pair_order(bank),
-                    recips[s * HALVES + h][:],
-                    MULT,
+                z = z_turned[(s // 4) * HALVES + h][:, :, :, 64 * quarter : 64 * (quarter + 1)].rearrange(
+                    "p u m (q e) -> p u m q e", e=2
                 )
+                if s in POOL_SLICES:
+                    numerator = numerators[(s * HALVES + h) % 8]
+                    nc.gpsimd.tensor_tensor(z, numerator[:], recips[s * HALVES + h][:], MULT)
+                else:
+                    nc.vector.tensor_tensor(z, pair_order(bank), recips[s * HALVES + h][:], MULT)
 
         def quantize_z(b, h, two_banks, copies):
             words = z_turned[b * HALVES + h][:].bitcast(F32)
@@ -294,7 +325,7 @@ def tile_list_flare_sector_score_kernel(
         loop_product(1)
         nc.vector.tensor_copy(g_scales[:], v_scales[:].indirect(idx[:]))
         nc.gpsimd.dma_start(out=g_scales_moved[0:100, :].bitcast(I32), in_=g_scales[4:104, :].bitcast(I32))
-        for page in loop_pages[3:]:
+        for page in region_pages + loop_pages[3:]:
             nc.gpsimd.memset(page[:], 0.0)
         loop_scatter(0)
         loop_scatter(1)
@@ -302,52 +333,73 @@ def tile_list_flare_sector_score_kernel(
         for a in range(2):
             nc.vector.tensor_copy(g_words[a][:], v_words[a][:].indirect(idx[:]))
         quantize_w2(3)
-        for s in range(2, SLICES):
+        for s in range(2, 4):
             loop_product(s)
-            loop_scatter(s)
-        for page in region_pages:
-            nc.gpsimd.memset(page[:], 0.0)
-        for s in range(SLICES):
-            region_product(s)
-        for s in range(SLICES):
-            engine = nc.vector if s == 0 else nc.gpsimd
-            engine.tensor_tensor(h1[:], y[s][:], tanh_y[s][:], MULT)
-            engine.tensor_tensor(y[s][:], h1[:], wg1_sb[:], MULT)
-        columns_from_rows(level_cols, level_rows, banks[REGION_BANKS[(SLICES - 1) % len(REGION_BANKS)]])
+        loop_scatter(2)
+        loop_values(3)
+        loop_scatter(3)
         for s in range(RING):
             load_quiet(s)
-        scalar_copies = (nc.scalar.copy, nc.scalar.copy)
-        held_banks = root_banks + turn_banks
-
-        for s in range(LEAD + 1):
-            reciprocal_of_denominator(s)
-        region_scatter(0)
         for s in range(SLICES):
-            if s + 1 < SLICES:
-                region_scatter(s + 1)
-            if s + LEAD + 1 < SLICES:
-                reciprocal_of_denominator(s + LEAD + 1)
-            quotient(s)
-            if s + RING < SLICES:
-                load_quiet(s + RING)
+            region_product(s)
+        for s in range(4, SLICES):
+            loop_product(s)
+        for s in range(4):
+            region_values(s)
+            region_scatter(s)
+            if s < 2:
+                numerator_sum(s)
+        columns_from_rows(level_cols, level_rows, banks[REGION_BANKS[(SLICES - 1) % len(REGION_BANKS)]])
+        scalar_copies = (nc.scalar.copy, nc.scalar.copy)
+        for s in range(4):
+            reciprocal_of_denominator(s)
+            loop_values(s + 4)
+            loop_scatter(s + 4)
             if s == 3:
-                for h in range(HALVES):
-                    quantize_z(0, h, turn_banks, scalar_copies)
-            if s == 4:
-                for i in range(4):
-                    score_pass(0, 1, i, sum_banks[2 + i % 2], True, True)
-                    nc.scalar.copy(out=first_pass[i][:], in_=sum_banks[2 + i % 2][:])
-            if s == 5:
-                for i in range(4):
-                    score_pass(0, 0, i, held_banks[i], True, False)
-
-        quantize_z(1, 0, sum_banks[0:2], (nc.scalar.copy, nc.vector.tensor_copy))
-        quantize_z(1, 1, sum_banks[2:4], scalar_copies)
+                numerator_sum(2)
+        region_values(4)
+        region_values(5)
+        numerator_sum(3)
+        quotient(0)
+        quotient(1)
+        quotient(2)
+        quotient(3, (0,))
+        region_h1(6)
+        quotient(3, (1,))
+        region_weighted(6)
+        for s in range(4, SLICES):
+            reciprocal_of_denominator(s)
+        region_scatter(4)
+        region_scatter(5)
+        quantize_z(0, 0, root_banks, scalar_copies)
+        numerator_sum(4)
+        region_h1(7)
+        quotient(4, (0,))
+        region_weighted(7)
+        quotient(4, (1,))
+        region_scatter(6)
+        quantize_z(0, 1, root_banks, scalar_copies)
+        numerator_sum(5)
+        quotient(5)
+        spare = turn_banks + root_banks
         for i in range(4):
-            score_pass(1, 0, i, held_banks[i], False, True)
-            nc.scalar.copy(out=staged[i][:], in_=held_banks[i][:])
+            score_pass(0, 1, i, spare[i], True, True)
+            nc.scalar.copy(out=first_pass[i][:], in_=spare[i][:])
+        region_scatter(7)
+        for s in range(6, SLICES):
+            numerator_sum(s)
+            quotient(s)
+
+        free_banks = turn_banks + root_banks
+        quantize_z(1, 0, turn_banks, (nc.scalar.copy, nc.vector.tensor_copy))
+        quantize_z(1, 1, root_banks, scalar_copies)
+        for i in range(4):
+            score_pass(0, 0, i, sum_banks[i], True, False)
+        for i in range(4):
+            score_pass(1, 0, i, sum_banks[i], False, True)
+            nc.scalar.copy(out=staged[i][:], in_=sum_banks[i][:])
             store_scores(0, i)
         for i in range(4):
-            score_pass(1, 1, i, sum_banks[i], True, True)
-            nc.vector.tensor_tensor(staged[4 + i][:], sum_banks[i][:], first_pass[i][:], ADD)
+            score_pass(1, 1, i, free_banks[i], True, True)
+            nc.vector.tensor_tensor(staged[4 + i][:], free_banks[i][:], first_pass[i][:], ADD)
             store_scores(1, i)

@@ -23,14 +23,14 @@ BANK = 512
 SLICES = H // P
 HALVES = T2 // BANK
 BLOCKS = BANK // P
-REGION_PAGES = 2
+REGION_PAGES = 3
+REGION_PAGE_OF = (0, 1, 0, 1, 0, 1, 2, 1)
 RING = 4
 W2_CHUNKS = ((0, 128), (128, 256), (256, 512), (512, 1024))
 KIB = 1024
-AHEAD = 4
+GROUPS = ((0,), (1,), (2,), (3,), (4, 5), (6, 7))
 FUSED = 3
 POOL_SLICES = (0, 1, 2, 3, 4, 5)
-LEAD = 3
 REGION_BANKS = (2, 3, 6, 7)
 
 
@@ -64,24 +64,39 @@ def tile_list_flare_sector_score_kernel(
 
         widths = [hi - lo for lo, hi in W2_CHUNKS]
         loop_pages = [placed("loop_page%d" % s, [P, T2], F32, 4 * s) for s in range(4)]
-        region_pages = [placed("region_page%d" % i, [P, T2], F32, (56, 128)[i]) for i in range(REGION_PAGES)]
+        region_pages = [placed("region_page%d" % i, [P, T2], F32, (56, 128, 154)[i]) for i in range(REGION_PAGES)]
         v_scales = placed("v_scales", [P, T], U8, 12)
         w2_codes = [placed("w2_codes%d" % c, [P, widths[c]], U32, (57, 129, 60, 52)[c]) for c in range(4)]
-        w2_plane = [placed("w2_plane%d" % c, [P, widths[c]], U8, (56, 128, 61, 62)[c]) for c in range(4)]
+        w2_plane = [placed("w2_plane%d" % c, [P, widths[c]], U8, (56, 154, 61, 62)[c]) for c in range(4)]
         w1_codes = placed("w1_codes", [P, 2, 2 * H], U8, 32)
         g_words = [placed("g_words%d" % a, [P, S], U32, 36 + 2 * a) for a in range(2)]
         v_words = [placed("v_words%d" % a, [P, T], U32, 40 + 8 * a) for a in range(2)]
-        abs_kib = [{2: 48, 3: 50}.get(s, 64 + 2 * s) for s in range(SLICES)]
-        h2_abs = [placed("h2_abs%d" % s, [P, S], F32, abs_kib[s]) for s in range(SLICES)]
-        pb_values = {s: placed("pb_values%d" % s, [P, S], F32, 112 + 2 * 3 if s == FUSED + 1 else abs_kib[s - 1]) for s in range(FUSED, SLICES)}
+        def grouped(name, kibs):
+            made = [placed("%s%d" % (name, g[0]), [P, len(g), S], F32, kib) for g, kib in zip(GROUPS, kibs)]
+            return {s: made[i] for i, g in enumerate(GROUPS) for s in g}
+
+        def of_slice(group_tiles, s):
+            return group_tiles[s][:, s % 2 if s >= 4 else 0, :]
+
+        h2_abs = grouped("h2_abs", (64, 66, 48, 50, 72, 76))
+        pb_values = {3: placed("pb_values3", [P, 1, S], F32, 48)}
+        for s, kib in ((4, 116), (6, 72)):
+            pb_values[s] = pb_values[s + 1] = placed("pb_values%d" % s, [P, 2, S], F32, kib)
+        y = grouped("y", (138, 140, 142, 144, 146, 150))
+        tanh_y = grouped("tanh_y", (112, 114, 116, 118, 120, 124))
+        pa_values = grouped("pa_values", (138, 140, 142, 144, 146, 150))
+        h1_single = placed("h1_single", [P, 1, S], F32, 50)
+        h1 = {s: h1_single for s in range(4)}
+        h1[4] = placed("h1_4", [P, 2, S], F32, 50)
+        h1[6] = placed("h1_6", [P, 2, S], F32, 28)
         quiet_sb = [placed("quiet_sb%d" % i, [P, T2], F32, (40, 44, 132, 68)[i]) for i in range(RING)]
-        h1_first = placed("h1_first", [P, S], F32, abs_kib[FUSED])
-        h1 = [h1_first] * 5 + [placed("h1_5", [P, S], F32, 112 + 2 * 4)] + [placed("h1_last", [P, S], F32, 16 + 2 * 6)] * 2
-        pa_values = [placed("pa_values%d" % s, [P, S], F32, {6: 16 + 2 * 7}.get(s, 138 + 2 * s)) for s in range(SLICES)]
-        numerators = [placed("numerator%d" % i, [P, 2, BLOCKS, 32, 2], F32, 16 + 2 * i) for i in range(8)]
-        recips = [placed("recip%d" % i, [P, 2, BLOCKS, 32, 2], F32, 80 + 2 * i) for i in range(SLICES * HALVES)]
-        z_turned = [placed("z_turned%d" % i, [P, 2, BLOCKS, 256], BF16, (32, 36, 0, 4)[i]) for i in range(2 * HALVES)]
-        tanh_y = [placed("tanh_y%d" % s, [P, S], F32, 112 + 2 * s) for s in range(SLICES)]
+        turned = [P, HALVES, 2, BLOCKS, 32, 2]
+        numerators = [placed("numerator%d" % s, turned, F32, (16, 20, 24, 28, 24, 8)[s]) for s in POOL_SLICES]
+        recips = [placed("recip%d" % s, turned, F32, 80 + 4 * s) for s in range(SLICES)]
+        z_first = placed("z_first", [P, HALVES, 2, BLOCKS, 256], BF16, 32)
+        z_last = [placed("z_last%d" % h, [P, 2, BLOCKS, 256], BF16, 4 * h) for h in range(HALVES)]
+        pairs_first = placed("pairs_first", [P, 4 * BANK], F32, 16)
+        codes_first = placed("codes_first", [P, T2], U32, 146)
         staged = [placed("staged%d" % s, [P, BANK], F32, 112 + 2 * s) for s in range(4 * HALVES)]
 
         w2_raw = [tile("w2_raw%d_" % c, [P, 4, widths[c]], F32) for c in range(4)]
@@ -103,12 +118,11 @@ def tile_list_flare_sector_score_kernel(
         level_rows = tile("level_rows", [P, P], F32)
         b2_cols = tile("b2_cols", [P, SLICES], F32)
         level_cols = tile("level_cols", [P, SLICES], F32)
-        y = [placed("y%d" % s, [P, S], F32, 138 + 2 * s) for s in range(SLICES)]
         roots = tiles("root", 2, [P, T2], F32)
-        z_pairs = tiles("z_pairs", HALVES, [P, 2 * BANK], F32)
-        z_codes = [placed("z_codes0", [P, BANK], U32, 138 + 2 * 5), placed("z_codes1", [P, BANK], U32, 16 + 2 * 7)]
-        z_codes = z_codes + tiles("z_codes_last", HALVES, [P, BANK], U32)
-        z_plane = tiles("z_plane", 2 * HALVES, [P, BANK], U8)
+        pairs_last = tiles("pairs_last", HALVES, [P, 2 * BANK], F32)
+        codes_last = tiles("codes_last", HALVES, [P, BANK], U32)
+        plane_first = tile("plane_first", [P, T2], U8)
+        plane_last = tiles("plane_last", HALVES, [P, BANK], U8)
 
         def zero_plane(t):
             nc.vector.memset(t.bitcast(I32), 0)
@@ -197,17 +211,20 @@ def tile_list_flare_sector_score_kernel(
                 start=True,
                 stop=True,
             )
-            nc.scalar.activation(h2_abs[s][:], bank[:], ACT.Abs, bias=b2_cols[:, s : s + 1])
+            nc.scalar.activation(of_slice(h2_abs, s), bank[:], ACT.Abs, bias=b2_cols[:, s : s + 1])
+
+        def for_group(weights, s):
+            return weights[:].unsqueeze(1).to_broadcast([P, 2 if s >= 4 else 1, S])
 
         def loop_values(s):
             engine = nc.vector if s == FUSED else nc.gpsimd
-            engine.tensor_tensor(pb_values[s][:], h2_abs[s][:], wg2_sb[:], MULT)
+            engine.tensor_tensor(pb_values[s][:], h2_abs[s][:], for_group(wg2_sb, s), MULT)
 
         def loop_scatter(s):
             if s < FUSED:
-                nc.vector.tensor_tensor(loop_pages[s % 4][:].indirect(idx4[:]), h2_abs[s][:], wg2_sb[:], MULT)
+                nc.vector.tensor_tensor(loop_pages[s % 4][:].indirect(idx4[:]), of_slice(h2_abs, s), wg2_sb[:], MULT)
             else:
-                nc.vector.tensor_copy(loop_pages[s % 4][:].indirect(idx4[:]), pb_values[s][:])
+                nc.vector.tensor_copy(loop_pages[s % 4][:].indirect(idx4[:]), of_slice(pb_values, s))
 
         def region_product(s):
             bank = banks[REGION_BANKS[s % len(REGION_BANKS)]]
@@ -221,15 +238,15 @@ def tile_list_flare_sector_score_kernel(
                     start=(a == 0),
                     stop=(a == 1),
                 )
-            nc.scalar.activation(tanh_y[s][:], bank[:], ACT.Tanh)
-            nc.scalar.copy(out=y[s][:], in_=bank[:])
+            nc.scalar.activation(of_slice(tanh_y, s), bank[:], ACT.Tanh)
+            nc.scalar.copy(out=of_slice(y, s), in_=bank[:])
 
         def pair_order(bank):
             return bank[:].rearrange("p (m q u e) -> p u m q e", m=BLOCKS, u=2, e=2)
 
         def reciprocal_of_denominator(s):
             root = roots[s % 2]
-            pair = sum_banks[0:2] if s % 4 == 3 else root_banks
+            pair = sum_banks[0:2] if s in (3, 7) else root_banks
             nc.scalar.activation(
                 root[:], loop_pages[s % 4][:], ACT.Abs_reciprocal_sqrt, bias=level_cols[:, s : s + 1]
             )
@@ -237,23 +254,27 @@ def tile_list_flare_sector_score_kernel(
                 for m in range(BLOCKS):
                     first = h * BANK + m * P
                     nc.tensor.transpose(pair[h][:, m * P : (m + 1) * P], root[:, first : first + P], ident[:])
-                nc.scalar.activation(recips[s * HALVES + h][:], pair_order(pair[h]), ACT.Square)
+                nc.scalar.activation(recips[s][:, h], pair_order(pair[h]), ACT.Square)
 
         def region_h1(s):
             nc.gpsimd.tensor_tensor(h1[s][:], y[s][:], tanh_y[s][:], MULT)
 
         def region_weighted(s):
-            nc.gpsimd.tensor_tensor(pa_values[s][:], h1[s][:], wg1_sb[:], MULT)
+            if s == 6:
+                for i in range(2):
+                    nc.gpsimd.tensor_tensor(pa_values[s][:, i, :], h1[s][:, i, :], wg1_sb[:], MULT)
+            else:
+                nc.gpsimd.tensor_tensor(pa_values[s][:], h1[s][:], for_group(wg1_sb, s), MULT)
 
         def region_values(s):
             region_h1(s)
             region_weighted(s)
 
         def region_scatter(s):
-            nc.vector.tensor_copy(region_pages[s % REGION_PAGES][:].indirect(idx3[:]), pa_values[s][:])
+            nc.vector.tensor_copy(region_pages[REGION_PAGE_OF[s]][:].indirect(idx3[:]), of_slice(pa_values, s))
 
         def numerator_sum(s):
-            terms = (quiet_sb[s % RING], region_pages[s % REGION_PAGES])
+            terms = (quiet_sb[s % RING], region_pages[REGION_PAGE_OF[s]])
             for h in range(HALVES):
                 bank = sum_banks[(HALVES if s == SLICES - 1 else 0) + h]
                 for term in range(2):
@@ -268,47 +289,48 @@ def tile_list_flare_sector_score_kernel(
                             stop=(term == 1 and m == BLOCKS - 1),
                         )
                 if s in POOL_SLICES:
-                    nc.scalar.copy(out=numerators[(s * HALVES + h) % 8][:], in_=pair_order(bank))
+                    nc.scalar.copy(out=numerators[s][:, h], in_=pair_order(bank))
             if s + RING < SLICES:
                 load_quiet(s + RING)
 
-        def quotient(s, halves=(0, 1)):
-            for h in halves:
-                bank = sum_banks[(HALVES if s == SLICES - 1 else 0) + h]
-                quarter = s % 4
-                z = z_turned[(s // 4) * HALVES + h][:, :, :, 64 * quarter : 64 * (quarter + 1)].rearrange(
-                    "p u m (q e) -> p u m q e", e=2
-                )
+        def quotient(s):
+            words = slice(64 * (s % 4), 64 * (s % 4 + 1))
+            if s < 4:
+                z = z_first[:, :, :, :, words].rearrange("p h u m (q e) -> p h u m q e", e=2)
+                nc.gpsimd.tensor_tensor(z, numerators[s][:], recips[s][:], MULT)
+                return
+            for h in range(HALVES):
+                z = z_last[h][:, :, :, words].rearrange("p u m (q e) -> p u m q e", e=2)
                 if s in POOL_SLICES:
-                    numerator = numerators[(s * HALVES + h) % 8]
-                    nc.gpsimd.tensor_tensor(z, numerator[:], recips[s * HALVES + h][:], MULT)
+                    nc.gpsimd.tensor_tensor(z, numerators[s][:, h], recips[s][:, h], MULT)
                 else:
-                    nc.vector.tensor_tensor(z, pair_order(bank), recips[s * HALVES + h][:], MULT)
+                    bank = sum_banks[(HALVES if s == SLICES - 1 else 0) + h]
+                    nc.vector.tensor_tensor(z, pair_order(bank), recips[s][:, h], MULT)
 
-        def quantize_z(b, h, two_banks, copies):
-            words = z_turned[b * HALVES + h][:].bitcast(F32)
+        def turn_back(z_half, pairs, two_banks, copies):
+            words = z_half.bitcast(F32)
             for j, bank in enumerate(two_banks):
                 for k in range(2):
                     for u in range(2):
                         first = (2 * k + u) * P
                         nc.tensor.transpose(bank[:, first : first + P], words[:, u, 2 * j + k, :], ident[:])
                 copies[j](
-                    out=z_pairs[h][:, j * BANK : (j + 1) * BANK].rearrange("p (k m u) -> p k m u", k=2, u=2),
+                    out=pairs[:, j * BANK : (j + 1) * BANK].rearrange("p (k m u) -> p k m u", k=2, u=2),
                     in_=bank[:].rearrange("p (k u m) -> p k m u", k=2, u=2),
                 )
-            nc.vector.quantize_mx(
-                out=z_codes[b * HALVES + h][:].bitcast(FP8X4),
-                scales=z_plane[b * HALVES + h][:],
-                in_=z_pairs[h][:].bitcast(BF16),
-            )
+
+        def quantize_z(codes, plane, pairs):
+            nc.vector.quantize_mx(out=codes[:].bitcast(FP8X4), scales=plane[:], in_=pairs[:].bitcast(BF16))
 
         def score_pass(b, h, i, bank, start, stop):
+            columns = slice(h * BANK, (h + 1) * BANK)
+            codes, plane = (codes_first[:, columns], plane_first[:, columns]) if b == 0 else (codes_last[h][:], plane_last[h][:])
             nc.tensor.matmul_mx(
                 out=bank[:],
                 lhsT=w3_codes[:, b, i * P : (i + 1) * P].bitcast(FP8X4),
                 lhsT_scale=w3_plane[:, b, i * P : (i + 1) * P],
-                rhs=z_codes[b * HALVES + h][:].bitcast(FP8X4),
-                rhs_scale=z_plane[b * HALVES + h][:],
+                rhs=codes.bitcast(FP8X4),
+                rhs_scale=plane,
                 start=start,
                 stop=stop,
             )
@@ -353,32 +375,25 @@ def tile_list_flare_sector_score_kernel(
         scalar_copies = (nc.scalar.copy, nc.scalar.copy)
         for s in range(4):
             reciprocal_of_denominator(s)
-            loop_values(s + 4)
+            if s % 2 == 0:
+                loop_values(s + 4)
             loop_scatter(s + 4)
-            if s == 3:
-                numerator_sum(2)
+        numerator_sum(2)
         region_values(4)
-        region_values(5)
         numerator_sum(3)
-        quotient(0)
-        quotient(1)
-        quotient(2)
-        quotient(3, (0,))
-        region_h1(6)
-        quotient(3, (1,))
-        region_weighted(6)
+        for s in range(4):
+            quotient(s)
+        region_values(6)
         for s in range(4, SLICES):
             reciprocal_of_denominator(s)
         region_scatter(4)
         region_scatter(5)
-        quantize_z(0, 0, root_banks, scalar_copies)
+        for h in range(HALVES):
+            turn_back(z_first[:, h], pairs_first[:, 2 * h * BANK : 2 * (h + 1) * BANK], root_banks, scalar_copies)
+        quantize_z(codes_first, plane_first, pairs_first)
         numerator_sum(4)
-        region_h1(7)
-        quotient(4, (0,))
-        region_weighted(7)
-        quotient(4, (1,))
+        quotient(4)
         region_scatter(6)
-        quantize_z(0, 1, root_banks, scalar_copies)
         numerator_sum(5)
         quotient(5)
         spare = turn_banks + root_banks
@@ -391,8 +406,10 @@ def tile_list_flare_sector_score_kernel(
             quotient(s)
 
         free_banks = turn_banks + root_banks
-        quantize_z(1, 0, turn_banks, (nc.scalar.copy, nc.vector.tensor_copy))
-        quantize_z(1, 1, root_banks, scalar_copies)
+        turn_back(z_last[0][:], pairs_last[0][:], turn_banks, (nc.scalar.copy, nc.vector.tensor_copy))
+        quantize_z(codes_last[0], plane_last[0], pairs_last[0])
+        turn_back(z_last[1][:], pairs_last[1][:], root_banks, scalar_copies)
+        quantize_z(codes_last[1], plane_last[1], pairs_last[1])
         for i in range(4):
             score_pass(0, 0, i, sum_banks[i], True, False)
         for i in range(4):

from contextlib import ExitStack

import concourse.mybir as mybir
from concourse.masks import make_identity

K, K2, H, N, T, T3, S, T2 = 1024, 512, 1024, 512, 2048, 1024, 512, 1024
FLOPS = 2 * (K * H * S + K2 * H * S + H * N * T2)

F32 = mybir.dt.float32
BF16 = mybir.dt.bfloat16
I32 = mybir.dt.int32
U32 = mybir.dt.uint32
U16 = mybir.dt.uint16
U8 = mybir.dt.uint8
FP8X4 = mybir.dt.float8_e4m3fn_x4
FP4X4 = mybir.dt.float4_e2m1fn_x4
ACT = mybir.ActivationFunctionType
MULT = mybir.AluOpType.mult
ADD = mybir.AluOpType.add

P = 128
BANK = 512
SLICES = H // P
HALVES = T2 // BANK
BLOCKS = BANK // P
REGION_PAGES = 3
REGION_PAGE_OF = (0, 1, 0, 1, 0, 1, 2, 1)
RING = 4
W2_CHUNKS = ((0, 128), (128, 256), (256, 512), (512, 1024))
KIB = 1024
GROUPS = ((0,), (1,), (2,), (3,), (4, 5), (6, 7))
FUSED = 3
POOL_SLICES = (0, 1, 2, 3, 4, 5)
REGION_BANKS = (2, 3, 6, 7)


def tile_list_flare_sector_score_kernel(
    tc, tab_words, tab_scales, tab2_words, tab2_scales, offs, offs2, offs3, offs4,
    w1_words, w1_scales, w2, b2, wg1, wg2, quiet, level, w3_words, w3_scales, out,
):
    nc = tc.nc
    with ExitStack() as ctx:
        lists = ctx.enter_context(tc.tile_pool(name="lists", bufs=1))
        sb = ctx.enter_context(tc.tile_pool(name="sb", bufs=1))
        reused = ctx.enter_context(tc.tile_pool(name="reused", bufs=1))
        ps = ctx.enter_context(tc.psum_pool(name="ps", bufs=1))

        def tiles(name, count, shape, dtype):
            return [sb.tile(shape, dtype, name="%s%d" % (name, i), align_bytes=64) for i in range(count)]

        def tile(name, shape, dtype):
            return tiles(name, 1, shape, dtype)[0]

        banks = [ps.tile([P, BANK], F32, name="bank%d" % i) for i in range(8)]
        turn_banks, root_banks, sum_banks = banks[0:2], banks[2:4], banks[4:8]

        idx = lists.tile([P, S // 16], U16, name="idx")
        idx2 = lists.tile([P, S // 16], U16, name="idx2")
        idx3 = lists.tile([P, S // 16], U16, name="idx3")
        idx4 = lists.tile([P, S // 16], U16, name="idx4")

        def placed(name, shape, dtype, kib):
            return reused.tile(shape, dtype, name=name, align_bytes=64, offset=kib * KIB)

        widths = [hi - lo for lo, hi in W2_CHUNKS]
        loop_pages = [placed("loop_page%d" % s, [P, T2], F32, 4 * s) for s in range(4)]
        region_pages = [placed("region_page%d" % i, [P, T2], F32, (56, 128, 154)[i]) for i in range(REGION_PAGES)]
        v_scales = placed("v_scales", [P, T], U8, 12)
        w2_codes = [placed("w2_codes%d" % c, [P, widths[c]], U32, (57, 129, 60, 52)[c]) for c in range(4)]
        w2_plane = [placed("w2_plane%d" % c, [P, widths[c]], U8, (56, 154, 61, 62)[c]) for c in range(4)]
        w1_codes = placed("w1_codes", [P, 2, 2 * H], U8, 32)
        g_words = [placed("g_words%d" % a, [P, S], U32, 36 + 2 * a) for a in range(2)]
        v_words = [placed("v_words%d" % a, [P, T], U32, 40 + 8 * a) for a in range(2)]
        def grouped(name, kibs):
            made = [placed("%s%d" % (name, g[0]), [P, len(g), S], F32, kib) for g, kib in zip(GROUPS, kibs)]
            return {s: made[i] for i, g in enumerate(GROUPS) for s in g}

        def of_slice(group_tiles, s):
            return group_tiles[s][:, s % 2 if s >= 4 else 0, :]

        h2_abs = grouped("h2_abs", (64, 66, 48, 50, 72, 76))
        pb_values = {3: placed("pb_values3", [P, 1, S], F32, 48)}
        for s, kib in ((4, 116), (6, 72)):
            pb_values[s] = pb_values[s + 1] = placed("pb_values%d" % s, [P, 2, S], F32, kib)
        y = grouped("y", (138, 140, 142, 144, 146, 150))
        tanh_y = grouped("tanh_y", (112, 114, 116, 118, 120, 124))
        pa_values = grouped("pa_values", (138, 140, 142, 144, 146, 150))
        h1_single = placed("h1_single", [P, 1, S], F32, 50)
        h1 = {s: h1_single for s in range(4)}
        h1[4] = placed("h1_4", [P, 2, S], F32, 50)
        h1[6] = placed("h1_6", [P, 2, S], F32, 28)
        quiet_sb = [placed("quiet_sb%d" % i, [P, T2], F32, (40, 44, 132, 68)[i]) for i in range(RING)]
        turned = [P, HALVES, 2, BLOCKS, 32, 2]
        numerators = [placed("numerator%d" % s, turned, F32, (16, 20, 24, 28, 24, 8)[s]) for s in POOL_SLICES]
        recips = [placed("recip%d" % s, turned, F32, 80 + 4 * s) for s in range(SLICES)]
        z_first = placed("z_first", [P, HALVES, 2, BLOCKS, 256], BF16, 32)
        z_last = [placed("z_last%d" % h, [P, 2, BLOCKS, 256], BF16, 4 * h) for h in range(HALVES)]
        pairs_first = placed("pairs_first", [P, 4 * BANK], F32, 16)
        codes_first = placed("codes_first", [P, T2], U32, 146)
        staged = [placed("staged%d" % s, [P, BANK], F32, 112 + 2 * s) for s in range(4 * HALVES)]

        w2_raw = [tile("w2_raw%d_" % c, [P, 4, widths[c]], F32) for c in range(4)]
        w2_bf = [tile("w2_bf%d_" % c, [P, widths[c], 4], BF16) for c in range(4)]
        first_pass = tiles("first_pass", 4, [P, BANK], F32)
        v2_words = tile("v2_words", [P, T3], U32)
        v2_scales = tile("v2_scales", [P, T3], U8)
        w1_plane = tile("w1_plane", [P, 2, H], U8)
        w3_codes = tile("w3_codes", [P, 2, N], U32)
        w3_plane = tile("w3_plane", [P, 2, N], U8)
        g2_words = tile("g2_words", [P, S], U32)
        g2_scales = tile("g2_scales", [P, S], U8)
        g_scales = tile("g_scales", [P, S], U8)
        g_scales_moved = tile("g_scales_moved", [P, S], U8)
        wg1_sb = tile("wg1_sb", [P, S], F32)
        wg2_sb = tile("wg2_sb", [P, S], F32)
        ident = tile("ident", [P, P], F32)
        b2_rows = tile("b2_rows", [P, P], F32)
        level_rows = tile("level_rows", [P, P], F32)
        b2_cols = tile("b2_cols", [P, SLICES], F32)
        level_cols = tile("level_cols", [P, SLICES], F32)
        roots = tiles("root", 2, [P, T2], F32)
        pairs_last = tiles("pairs_last", HALVES, [P, 2 * BANK], F32)
        codes_last = tiles("codes_last", HALVES, [P, BANK], U32)
        plane_first = tile("plane_first", [P, T2], U8)
        plane_last = tiles("plane_last", HALVES, [P, BANK], U8)

        def zero_plane(t):
            nc.vector.memset(t.bitcast(I32), 0)

        def load_scale_rows(dst_of_quadrant, src_of_quadrant):
            for q in range(4):
                nc.sync.dma_start(out=dst_of_quadrant(q).bitcast(I32), in_=src_of_quadrant(q).bitcast(I32))

        def load_words(dst, src):
            nc.sync.dma_start(out=dst.bitcast(I32), in_=src.bitcast(I32))

        def load_w2(c):
            lo, hi = W2_CHUNKS[c]
            nc.sync.dma_start(out=w2_raw[c][:], in_=w2[:, lo:hi].rearrange("(p j) c -> p j c", j=4))

        def load_quiet(s):
            nc.sync.dma_start(out=quiet_sb[s % RING][:], in_=quiet[s * P : (s + 1) * P, :])

        nc.gpsimd.memset(v_scales[:].bitcast(I32), 0)
        make_identity(nc, ident[:])
        zero_plane(w1_plane[:].rearrange("p a c -> p (a c)"))
        zero_plane(g_scales_moved[:])
        zero_plane(w3_plane[:].rearrange("p a c -> p (a c)"))
        for page in loop_pages[0:3]:
            nc.vector.memset(page[:], 0.0)

        def load_rows_on_all_partitions(rows, vector):
            nc.sync.dma_start(
                out=rows[:], in_=vector.rearrange("(s p) -> s p", p=P).unsqueeze(0).to_broadcast([P // SLICES, SLICES, P])
            )

        nc.sync.dma_start(idx2[:], offs2)
        load_scale_rows(
            lambda q: v2_scales[32 * q : 32 * (q + 1), :],
            lambda q: tab2_scales[0, 4 * q : 4 * q + 4, :].unsqueeze(0).to_broadcast([8, 4, T3]),
        )
        load_words(v2_words[:], tab2_words[0].rearrange("p t i -> p (t i)"))
        load_w2(0)
        load_rows_on_all_partitions(b2_rows, b2)
        load_w2(1)
        nc.sync.dma_start(idx[:], offs)
        load_scale_rows(lambda q: v_scales[32 * q : 32 * q + 8, :], lambda q: tab_scales[:, 4 * q : 4 * q + 4, :])
        nc.sync.dma_start(out=wg2_sb[:], in_=wg2)
        nc.sync.dma_start(idx4[:], offs4)
        load_w2(2)
        load_w2(3)
        load_words(v_words[0][:], tab_words[0].rearrange("p t i -> p (t i)"))
        load_words(v_words[1][:], tab_words[1].rearrange("p t i -> p (t i)"))
        load_words(w1_codes[:], w1_words.rearrange("a p c -> p a c"))
        load_scale_rows(
            lambda q: w1_plane[32 * q : 32 * q + 4, :, :],
            lambda q: w1_scales[:, 4 * q : 4 * q + 4, :].rearrange("a r c -> r a c"),
        )
        load_rows_on_all_partitions(level_rows, level)
        nc.sync.dma_start(idx3[:], offs3)
        nc.sync.dma_start(out=wg1_sb[:], in_=wg1)
        load_words(w3_codes[:], w3_words.rearrange("a p c i -> p a (c i)"))
        load_scale_rows(
            lambda q: w3_plane[32 * q : 32 * q + 4, :, :],
            lambda q: w3_scales[:, 4 * q : 4 * q + 4, :].rearrange("a r c -> r a c"),
        )

        def quantize_w2(c):
            nc.scalar.copy(
                out=w2_bf[c][:].rearrange("p (c i) j -> p c j i", i=4),
                in_=w2_raw[c][:].rearrange("p j (c i) -> p c j i", i=4),
            )
            nc.vector.quantize_mx(
                out=w2_codes[c][:].bitcast(FP8X4), scales=w2_plane[c][:], in_=w2_bf[c][:].rearrange("p c j -> p (c j)")
            )

        def columns_from_rows(cols, rows, bank):
            nc.tensor.transpose(bank[:, 0:P], rows[:], ident[:])
            nc.scalar.copy(out=cols[:], in_=bank[:, 0:SLICES])

        def loop_product(s):
            c = [i for i, (lo, hi) in enumerate(W2_CHUNKS) if lo <= s * P < hi][0]
            first = s * P - W2_CHUNKS[c][0]
            bank = turn_banks[s % 2]
            nc.tensor.matmul_mx(
                out=bank[:],
                lhsT=w2_codes[c][:, first : first + P].bitcast(FP8X4),
                lhsT_scale=w2_plane[c][:, first : first + P],
                rhs=g2_words[:].bitcast(FP8X4),
                rhs_scale=g2_scales[:],
                start=True,
                stop=True,
            )
            nc.scalar.activation(of_slice(h2_abs, s), bank[:], ACT.Abs, bias=b2_cols[:, s : s + 1])

        def for_group(weights, s):
            return weights[:].unsqueeze(1).to_broadcast([P, 2 if s >= 4 else 1, S])

        def loop_values(s):
            engine = nc.vector if s == FUSED else nc.gpsimd
            engine.tensor_tensor(pb_values[s][:], h2_abs[s][:], for_group(wg2_sb, s), MULT)

        def loop_scatter(s):
            if s < FUSED:
                nc.vector.tensor_tensor(loop_pages[s % 4][:].indirect(idx4[:]), of_slice(h2_abs, s), wg2_sb[:], MULT)
            else:
                nc.vector.tensor_copy(loop_pages[s % 4][:].indirect(idx4[:]), of_slice(pb_values, s))

        def region_product(s):
            bank = banks[REGION_BANKS[s % len(REGION_BANKS)]]
            for a, plane in enumerate((g_scales, g_scales_moved)):
                nc.tensor.matmul_mx(
                    out=bank[:],
                    lhsT=w1_codes[:, a, 2 * s * P : 2 * (s + 1) * P].bitcast(FP4X4),
                    lhsT_scale=w1_plane[:, a, s * P : (s + 1) * P],
                    rhs=g_words[a][:].bitcast(FP8X4),
                    rhs_scale=plane[:],
                    start=(a == 0),
                    stop=(a == 1),
                )
            nc.scalar.activation(of_slice(tanh_y, s), bank[:], ACT.Tanh)
            nc.scalar.copy(out=of_slice(y, s), in_=bank[:])

        def pair_order(bank):
            return bank[:].rearrange("p (m q u e) -> p u m q e", m=BLOCKS, u=2, e=2)

        def reciprocal_of_denominator(s):
            root = roots[s % 2]
            pair = sum_banks[0:2] if s in (3, 7) else root_banks
            nc.scalar.activation(
                root[:], loop_pages[s % 4][:], ACT.Abs_reciprocal_sqrt, bias=level_cols[:, s : s + 1]
            )
            for h in range(HALVES):
                for m in range(BLOCKS):
                    first = h * BANK + m * P
                    nc.tensor.transpose(pair[h][:, m * P : (m + 1) * P], root[:, first : first + P], ident[:])
                nc.scalar.activation(recips[s][:, h], pair_order(pair[h]), ACT.Square)

        def region_h1(s):
            nc.gpsimd.tensor_tensor(h1[s][:], y[s][:], tanh_y[s][:], MULT)

        def region_weighted(s):
            if s == 6:
                for i in range(2):
                    nc.gpsimd.tensor_tensor(pa_values[s][:, i, :], h1[s][:, i, :], wg1_sb[:], MULT)
            else:
                nc.gpsimd.tensor_tensor(pa_values[s][:], h1[s][:], for_group(wg1_sb, s), MULT)

        def region_values(s):
            region_h1(s)
            region_weighted(s)

        def region_scatter(s):
            nc.vector.tensor_copy(region_pages[REGION_PAGE_OF[s]][:].indirect(idx3[:]), of_slice(pa_values, s))

        def numerator_sum(s):
            terms = (quiet_sb[s % RING], region_pages[REGION_PAGE_OF[s]])
            for h in range(HALVES):
                bank = sum_banks[(HALVES if s == SLICES - 1 else 0) + h]
                for term in range(2):
                    for m in range(BLOCKS):
                        first = h * BANK + m * P
                        nc.tensor.matmul(
                            bank[:, m * P : (m + 1) * P],
                            lhsT=terms[term][:, first : first + P],
                            rhs=ident[:],
                            is_transpose=True,
                            start=(term == 0 and m == 0),
                            stop=(term == 1 and m == BLOCKS - 1),
                        )
                if s in POOL_SLICES:
                    nc.scalar.copy(out=numerators[s][:, h], in_=pair_order(bank))
            if s + RING < SLICES:
                load_quiet(s + RING)

        def quotient(s):
            words = slice(64 * (s % 4), 64 * (s % 4 + 1))
            if s < 4:
                z = z_first[:, :, :, :, words].rearrange("p h u m (q e) -> p h u m q e", e=2)
                nc.gpsimd.tensor_tensor(z, numerators[s][:], recips[s][:], MULT)
                return
            for h in range(HALVES):
                z = z_last[h][:, :, :, words].rearrange("p u m (q e) -> p u m q e", e=2)
                if s in POOL_SLICES:
                    nc.gpsimd.tensor_tensor(z, numerators[s][:, h], recips[s][:, h], MULT)
                else:
                    bank = sum_banks[(HALVES if s == SLICES - 1 else 0) + h]
                    nc.vector.tensor_tensor(z, pair_order(bank), recips[s][:, h], MULT)

        def turn_back(z_half, pairs, two_banks, copies):
            words = z_half.bitcast(F32)
            for j, bank in enumerate(two_banks):
                for k in range(2):
                    for u in range(2):
                        first = (2 * k + u) * P
                        nc.tensor.transpose(bank[:, first : first + P], words[:, u, 2 * j + k, :], ident[:])
                copies[j](
                    out=pairs[:, j * BANK : (j + 1) * BANK].rearrange("p (k m u) -> p k m u", k=2, u=2),
                    in_=bank[:].rearrange("p (k u m) -> p k m u", k=2, u=2),
                )

        def quantize_z(codes, plane, pairs):
            nc.vector.quantize_mx(out=codes[:].bitcast(FP8X4), scales=plane[:], in_=pairs[:].bitcast(BF16))

        def score_pass(b, h, i, bank, start, stop):
            columns = slice(h * BANK, (h + 1) * BANK)
            codes, plane = (codes_first[:, columns], plane_first[:, columns]) if b == 0 else (codes_last[h][:], plane_last[h][:])
            nc.tensor.matmul_mx(
                out=bank[:],
                lhsT=w3_codes[:, b, i * P : (i + 1) * P].bitcast(FP8X4),
                lhsT_scale=w3_plane[:, b, i * P : (i + 1) * P],
                rhs=codes.bitcast(FP8X4),
                rhs_scale=plane,
                start=start,
                stop=stop,
            )

        def store_scores(h, i):
            nc.sync.dma_start(out=out[i * P : (i + 1) * P, h * BANK : (h + 1) * BANK], in_=staged[4 * h + i][:])

        nc.vector.tensor_copy(g2_scales[:], v2_scales[:].indirect(idx2[:]))
        nc.vector.tensor_copy(g2_words[:], v2_words[:].indirect(idx2[:]))
        quantize_w2(0)
        columns_from_rows(b2_cols, b2_rows, turn_banks[1])
        loop_product(0)
        quantize_w2(1)
        loop_product(1)
        nc.vector.tensor_copy(g_scales[:], v_scales[:].indirect(idx[:]))
        nc.gpsimd.dma_start(out=g_scales_moved[0:100, :].bitcast(I32), in_=g_scales[4:104, :].bitcast(I32))
        for page in region_pages + loop_pages[3:]:
            nc.gpsimd.memset(page[:], 0.0)
        loop_scatter(0)
        loop_scatter(1)
        quantize_w2(2)
        for a in range(2):
            nc.vector.tensor_copy(g_words[a][:], v_words[a][:].indirect(idx[:]))
        quantize_w2(3)
        for s in range(2, 4):
            loop_product(s)
        loop_scatter(2)
        loop_values(3)
        loop_scatter(3)
        for s in range(RING):
            load_quiet(s)
        for s in range(SLICES):
            region_product(s)
        for s in range(4, SLICES):
            loop_product(s)
        for s in range(4):
            region_values(s)
            region_scatter(s)
            if s < 2:
                numerator_sum(s)
        columns_from_rows(level_cols, level_rows, banks[REGION_BANKS[(SLICES - 1) % len(REGION_BANKS)]])
        scalar_copies = (nc.scalar.copy, nc.scalar.copy)
        for s in range(4):
            reciprocal_of_denominator(s)
            if s % 2 == 0:
                loop_values(s + 4)
            loop_scatter(s + 4)
        numerator_sum(2)
        region_values(4)
        numerator_sum(3)
        for s in range(4):
            quotient(s)
        region_values(6)
        for s in range(4, SLICES):
            reciprocal_of_denominator(s)
        region_scatter(4)
        region_scatter(5)
        for h in range(HALVES):
            turn_back(z_first[:, h], pairs_first[:, 2 * h * BANK : 2 * (h + 1) * BANK], root_banks, scalar_copies)
        quantize_z(codes_first, plane_first, pairs_first)
        numerator_sum(4)
        quotient(4)
        region_scatter(6)
        numerator_sum(5)
        quotient(5)
        spare = turn_banks + root_banks
        for i in range(4):
            score_pass(0, 1, i, spare[i], True, True)
            nc.scalar.copy(out=first_pass[i][:], in_=spare[i][:])
        region_scatter(7)
        for s in range(6, SLICES):
            numerator_sum(s)
            quotient(s)

        free_banks = turn_banks + root_banks
        turn_back(z_last[0][:], pairs_last[0][:], turn_banks, (nc.scalar.copy, nc.vector.tensor_copy))
        quantize_z(codes_last[0], plane_last[0], pairs_last[0])
        turn_back(z_last[1][:], pairs_last[1][:], root_banks, scalar_copies)
        quantize_z(codes_last[1], plane_last[1], pairs_last[1])
        for i in range(4):
            score_pass(0, 0, i, sum_banks[i], True, False)
        for i in range(4):
            score_pass(1, 0, i, sum_banks[i], False, True)
            nc.scalar.copy(out=staged[i][:], in_=sum_banks[i][:])
            store_scores(0, i)
        for i in range(4):
            score_pass(1, 1, i, free_banks[i], True, True)
            nc.vector.tensor_tensor(staged[4 + i][:], free_banks[i][:], first_pass[i][:], ADD)
            store_scores(1, i)
